import numpy as np
import ml_dtypes


def mxq(x, axis, fmt="e4m3"):
    dtype, down = {"e4m3": (ml_dtypes.float8_e4m3fn, 7), "e5m2": (ml_dtypes.float8_e5m2, 14)}[fmt]
    v = np.moveaxis(np.asarray(x, np.float32).astype(ml_dtypes.bfloat16).astype(np.float64), axis, -1)
    blocks = v.reshape(v.shape[:-1] + (-1, 32))
    amax = np.abs(blocks).max(-1, keepdims=True)
    byte = np.maximum(np.where(amax > 0, np.frexp(amax)[1] - 1 + 127, 0) - down, 1)
    scale = np.exp2(byte - 127.0)
    codes = (blocks / scale).astype(np.float32).astype(dtype).astype(np.float64)
    return np.moveaxis((codes * scale).reshape(v.shape), -1, axis)


WIDE = False


def mx_kscale(k):
    if not WIDE:
        return np.ones(k)
    levels = np.array([10, -10, 5, -5, 0])
    if k % 512:
        return np.exp2(np.random.permutation(np.resize(levels, k // 32))).repeat(32)
    a = np.empty((k // 512, 16))
    for p in range(k // 512):
        a[p, :8] = np.random.permutation(np.resize(levels, 8))
        for g in range(8):
            far = levels[np.abs(levels - a[p, g]) >= 10]
            a[p, g + 8] = far[np.random.randint(len(far))]
    return np.exp2(a.ravel()).repeat(32)


def f64(x):
    return np.asarray(x).astype(np.float64)


def striped(idx):
    return np.tile(idx.reshape(-1, 16).T, (8, 1)).astype(np.uint16)


def unstriped(offs):
    return offs[:16].T.reshape(-1).astype(np.int64)


def striped8(idx):
    return np.concatenate([x.reshape(-1, 16).T for x in idx]).astype(np.uint16)


def runs(offs, k):
    lists = np.stack([offs[16 * r : 16 * r + 16].T.reshape(-1) for r in range(8)]).astype(np.int64)
    return lists[np.arange(k) % 512 // 64]


def pack_weight(w):
    k, n = w.shape
    w = f64(np.asarray(w, np.float32).astype(ml_dtypes.bfloat16)).reshape(k // 32, 32, n)
    amax = np.abs(w).max(1)
    byte = np.clip(np.where(amax > 0, np.frexp(amax)[1] - 1 + 127 - 7, 1), 1, 254)
    scaled = (w * np.exp2(127.0 - byte)[:, None, :]).reshape(k, n).astype(np.float32)
    words = np.ascontiguousarray(scaled.reshape(k // 512, 128, 4, n).transpose(0, 1, 3, 2)).astype(ml_dtypes.float8_e4m3fn).view(np.uint8)
    return words, np.ascontiguousarray(byte.astype(np.uint8).reshape(k // 512, 16, n))


def unpack_weight(words, scales):
    g, p, n, _ = words.shape
    vals = np.ascontiguousarray(words).view(ml_dtypes.float8_e4m3fn).astype(np.float64) * np.repeat(np.exp2(scales.astype(np.float64) - 127.0), 8, axis=1)[..., None]
    return vals.transpose(0, 1, 3, 2).reshape(g * 512, n)


E2M1 = np.array([0.0, 0.5, 1.0, 1.5, 2.0, 3.0, 4.0, 6.0, -0.0, -0.5, -1.0, -1.5, -2.0, -3.0, -4.0, -6.0])


def pack_fp4(w):
    k, n = w.shape
    w = f64(np.asarray(w, np.float32).astype(ml_dtypes.bfloat16)).reshape(k // 32, 32, n)
    amax = np.abs(w).max(1)
    mant, ex = np.frexp(amax / 6.0)
    byte = np.clip(np.where(amax > 0, np.where(mant > 0.5, ex, ex - 1) + 127, 1), 1, 254)
    scaled = (w * np.exp2(127.0 - byte)[:, None, :]).reshape(k, n).astype(np.float32)
    c = np.ascontiguousarray(scaled.reshape(k // 512, 128, 4, n).transpose(0, 1, 3, 2)).astype(ml_dtypes.float4_e2m1fn).view(np.uint8) & 0xF
    words = (c[..., 0::2] | (c[..., 1::2] << 4)).reshape(k // 512, 128, 2 * n)
    return np.ascontiguousarray(words), np.ascontiguousarray(byte.astype(np.uint8).reshape(k // 512, 16, n))


def unpack_fp4(words, scales):
    g, _, n = scales.shape
    words = np.ascontiguousarray(words).reshape(g, 128, n, 2)
    nib = np.empty((g, 128, n, 4), np.uint8)
    nib[..., 0::2] = words & 0xF
    nib[..., 1::2] = words >> 4
    vals = E2M1[nib] * np.repeat(np.exp2(scales.astype(np.float64) - 127.0), 8, axis=1)[..., None]
    return vals.transpose(0, 1, 3, 2).reshape(g * 512, n)


def planes(y):
    n, m = y.shape
    v = y.astype(np.float32).astype(ml_dtypes.bfloat16).astype(np.float64).reshape(n // 32, 32, m)
    top = np.abs(v).max(1)
    byte = np.clip(np.where(top > 0, np.frexp(top)[1] - 1 + 127 - 7, 1), 1, 254)
    codes = (v * np.exp2(127.0 - byte)[:, None, :]).reshape(n, m).astype(np.float32).astype(ml_dtypes.float8_e4m3fn).view(np.uint8)
    words = codes.reshape(n // 512, 128, 4, m).transpose(0, 1, 3, 2)
    return np.ascontiguousarray(words), np.ascontiguousarray(byte.astype(np.uint8).reshape(n // 512, 16, m))


K, T, S, H, C, W = 512, 2048, 512, 512, 512, 256


def setup_inputs():
    n = np.random.standard_normal
    s = mx_kscale(K)[:, None]
    packed_xT = pack_weight(n((K, T)) * s)
    packed_w1 = pack_fp4(n((K, H)) / np.sqrt(K) / s)
    return {
        "x_words": packed_xT[0],
        "x_scales": packed_xT[1],
        "w1_words": packed_w1[0],
        "w1_scales": packed_w1[1],
        "gs": (np.random.uniform(0.5, 1.5, (K, 1)) / s).astype(np.float32),
        "wb": (n((K, S)) / np.sqrt(K) / s).astype(np.float32),
        "offs": striped(np.random.permutation(T)[:S]),
        "n1": striped(np.random.permutation(S)),
        "n2": striped(np.random.permutation(S)),
        "cand": striped(np.random.permutation(T)[:C]),
        "cb": striped(np.random.permutation(T)[:C]),
        "n3": striped8(np.stack([np.random.permutation(S)[:W] for _ in range(8)])),
        "n4": striped8(np.stack([np.random.permutation(S)[:W] for _ in range(8)])),
    }


def reference(x_words, x_scales, w1_words, w1_scales, gs, wb, offs, n1, n2, cand, cb, n3, n4):
    x_cb = unpack_weight(x_words, x_scales)[:, unstriped(cb)]
    b = x_cb.T @ mxq(f64(wb), 0, "e4m3")
    x_cand = unpack_weight(x_words, x_scales)[:, unstriped(cand)]
    xq = unpack_weight(x_words, x_scales)[:, unstriped(offs)]
    y = unpack_fp4(w1_words, w1_scales).T @ xq
    st = np.maximum(y, y[:, unstriped(n1)])
    z = f64(gs) * (np.minimum(st, st[:, unstriped(n2)]))
    a = 0.0625 * ((x_cand.T @ mxq(z, 0, "e4m3")))
    ra = b[np.arange(C)[:, None], runs(n4, C)] - (0.5 * (a[np.arange(C)[:, None], runs(n3, C)]))
    out = a.copy()
    out[np.arange(C)[:, None], runs(n3, C)] = ra
    return (out,) + planes(out)

@@ -1,0 +1,185 @@
+from contextlib import ExitStack
+
+import concourse.mybir as mybir
+
+F32 = mybir.dt.float32
+BF16 = mybir.dt.bfloat16
+I32 = mybir.dt.int32
+U32 = mybir.dt.uint32
+U16 = mybir.dt.uint16
+U8 = mybir.dt.uint8
+FP8X4 = mybir.dt.float8_e4m3fn_x4
+FP4X4 = mybir.dt.float4_e2m1fn_x4
+ALU = mybir.AluOpType
+COPY = mybir.ActivationFunctionType.Copy
+
+P = 128
+PACK = 4
+T = 2048
+S = 512
+W = 256
+SPARE = 16
+FLOPS = 3 * 2 * 512 * 512 * 512
+
+
+def tile_picked_cdswputbhopmn_none_po_kernel(
+    tc, x_words, x_scales, w1_words, w1_scales, gs, wb, offs, n1, n2, cand, cb, n3, n4, out_0, out_1, out_2
+):
+    nc = tc.nc
+    with ExitStack() as ctx:
+        lists = ctx.enter_context(tc.tile_pool(name="lists", bufs=1))
+        keep = ctx.enter_context(tc.tile_pool(name="keep", bufs=1))
+        psum = ctx.enter_context(tc.psum_pool(name="psum", bufs=1))
+
+        def sb(name, shape, dtype):
+            return keep.tile(shape, dtype, name=name, align_bytes=64)
+
+        def load_list(name, src):
+            tile = lists.tile(list(src.shape), U16, name=name)
+            nc.sync.dma_start(tile[:], src)
+            return tile
+
+        def load_scale_rows(tile, src):
+            for q in range(4):
+                nc.sync.dma_start(tile[32 * q : 32 * q + 4, :].bitcast(I32), src[0, 4 * q : 4 * q + 4, :].bitcast(I32))
+
+        x_s = sb("x_s", [P, T], U8)
+        w1_s = sb("w1_s", [P, S], U8)
+        nc.vector.memset(x_s[:].bitcast(I32), 0)
+        nc.gpsimd.memset(w1_s[:].bitcast(I32), 0)
+        x_w = sb("x_w", [P, T], I32)
+        x_src = x_words[0].rearrange("p n t -> p (n t)").bitcast(I32)
+        nc.sync.dma_start(x_w[:, : T // 2], x_src[:, : T // 2])
+        load_scale_rows(x_s, x_scales)
+        offs_t = load_list("offs_t", offs)
+        w1_w = sb("w1_w", [P, 2 * S], U8)
+        nc.sync.dma_start(w1_w[:].bitcast(I32), w1_words[0].bitcast(I32))
+        nc.sync.dma_start(x_w[:, T // 2 :], x_src[:, T // 2 :])
+        load_scale_rows(w1_s, w1_scales)
+        cand_t = load_list("cand_t", cand)
+        cb_t = load_list("cb_t", cb)
+        n1_t = load_list("n1_t", n1)
+        wb_raw = sb("wb_raw", [P, PACK, S], F32)
+        nc.sync.dma_start(wb_raw[:], wb.rearrange("(p j) c -> p j c", j=PACK))
+        n2_t = load_list("n2_t", n2)
+        gs_t = sb("gs_t", [P, PACK], F32)
+        nc.sync.dma_start(gs_t[:], gs.rearrange("(p j) o -> p (j o)", j=PACK))
+        n4_t = load_list("n4_t", n4)
+        n3_t = load_list("n3_t", n3)
+
+        y_sb = [sb(f"y{t}", [P, S + SPARE], F32) for t in range(PACK)]
+        st_sb = [sb(f"st{t}", [P, S + SPARE], F32) for t in range(PACK)]
+        for t in range(PACK):
+            nc.gpsimd.memset(y_sb[t][:, S:], 0.0)
+            nc.gpsimd.memset(st_sb[t][:, S:], 0.0)
+
+        xq_s = sb("xq_s", [P, S], U8)
+        nc.vector.tensor_copy(xq_s[:], x_s[:].indirect(offs_t[:]))
+        w1_wd = sb("w1_wd", [P, 2 * S], U8)
+        nc.vector.tensor_copy(
+            w1_wd[:].rearrange("p (t m e) -> p t m e", t=PACK, e=2), w1_w[:].rearrange("p (m t e) -> p t m e", t=PACK, e=2)
+        )
+        w1_sd = sb("w1_sd", [P, S], U8)
+        nc.vector.tensor_copy(w1_sd[:].rearrange("p (t m) -> p t m", t=PACK), w1_s[:].rearrange("p (m t) -> p t m", t=PACK))
+        xq_w = sb("xq_w", [P, S], U32)
+        nc.vector.tensor_copy(xq_w[:], x_w[:].bitcast(U32).indirect(offs_t[:]))
+
+        def dealt_columns(name, picks):
+            words = sb(name + "_w", [P, S], U32)
+            nc.vector.tensor_copy(words[:].rearrange("p (t m) -> p m t", t=PACK), x_w[:].bitcast(U32).indirect(picks[:]))
+            raw = sb(name + "_raw", [P, S], U8)
+            nc.vector.tensor_copy(raw[:], x_s[:].indirect(picks[:]))
+            scales = sb(name + "_s", [P, S], U8)
+            nc.vector.tensor_copy(scales[:].rearrange("p (t m) -> p t m", t=PACK), raw[:].rearrange("p (m t) -> p t m", t=PACK))
+            return words, scales
+
+        def interleave(engine_copy, dst, src, c0, c1):
+            engine_copy(
+                dst[:, c0:c1, :].rearrange("p (c i) t -> p c t i", i=4),
+                src[:, :, c0:c1].rearrange("p t (c i) -> p c t i", i=4),
+            )
+
+        def quantize(name, grouped):
+            codes = sb(name + "_codes", [P, S], I32)
+            scales = sb(name + "_scales", [P, S], U8)
+            nc.vector.quantize_mx(out=codes[:].bitcast(FP8X4), scales=scales[:], in_=grouped[:].rearrange("p c t -> p (c t)"))
+            return codes, scales
+
+        def product(bank, t, words, scales, codes, code_scales):
+            cols = slice(t * P, (t + 1) * P)
+            nc.tensor.matmul_mx(
+                out=bank[:], lhsT=words[:, cols].bitcast(FP8X4), lhsT_scale=scales[:, cols],
+                rhs=codes[:].bitcast(FP8X4), rhs_scale=code_scales[:], start=True, stop=True,
+            )
+
+        y_ps = [psum.tile([P, S], F32, name=f"y_ps{t}", tag=f"ya{t}") for t in range(PACK)]
+        for t in range(PACK):
+            nc.tensor.matmul_mx(
+                out=y_ps[t][:], lhsT=w1_wd[:, 2 * P * t : 2 * P * (t + 1)].bitcast(FP4X4), lhsT_scale=w1_sd[:, P * t : P * (t + 1)],
+                rhs=xq_w[:].bitcast(FP8X4), rhs_scale=xq_s[:], start=True, stop=True,
+            )
+
+        cand_w, cand_s = dealt_columns("cand", cand_t)
+        cb_w, cb_s = dealt_columns("cb", cb_t)
+
+        g1 = [sb(f"g1_{t}", [P, S], F32) for t in range(PACK)]
+        for t in range(PACK):
+            nc.scalar.copy(y_sb[t][:, :S], y_ps[t][:])
+            nc.scalar.activation(g1[t][:], y_sb[t][:].indirect(n1_t[:]), COPY)
+        for t in range(PACK):
+            nc.vector.tensor_tensor(st_sb[t][:, :S], y_sb[t][:, :S], g1[t][:], ALU.max)
+
+        wb_il = sb("wb_il", [P, S, PACK], BF16)
+        interleave(nc.vector.tensor_copy, wb_il, wb_raw, 0, S)
+        wb_c, wb_s = quantize("wb", wb_il)
+        b_ps = [psum.tile([P, S], F32, name=f"b_ps{t}") for t in range(PACK)]
+        for t in range(PACK):
+            product(b_ps[t], t, cb_w, cb_s, wb_c, wb_s)
+
+        g2 = [sb(f"g2_{t}", [P, S], F32) for t in range(PACK)]
+        for t in range(PACK - 1):
+            nc.scalar.activation(g2[t][:], st_sb[t][:].indirect(n2_t[:]), COPY)
+        for h in range(2):
+            nc.vector.tensor_copy(g2[3][:, h * W : (h + 1) * W], st_sb[3][:].indirect(n2_t[:, 16 * h : 16 * (h + 1)]))
+        z_pl = sb("z_pl", [P, PACK, S], BF16)
+        mn = [sb(f"mn_{t}", [P, S], F32) for t in range(PACK)]
+        for t in (0, 3, 1, 2):
+            nc.vector.tensor_tensor(mn[t][:], st_sb[t][:, :S], g2[t][:], ALU.min)
+            nc.vector.tensor_scalar(z_pl[:, t, :], mn[t][:], gs_t[:, t : t + 1], None, ALU.mult)
+
+        z_il = sb("z_il", [P, S, PACK], BF16)
+        interleave(nc.vector.tensor_copy, z_il, z_pl, 0, S)
+        z_c, z_s = quantize("z", z_il)
+        a_ps = [psum.tile([P, S], F32, name=f"a_ps{t}", tag=f"ya{t}") for t in range(PACK)]
+        for t in range(PACK):
+            product(a_ps[t], t, cand_w, cand_s, z_c, z_s)
+
+        b_sb = [sb(f"b{t}", [P, S], F32) for t in range(PACK)]
+        g4 = [sb(f"g4_{t}", [P, W], F32) for t in range(PACK)]
+        for t in range(PACK):
+            nc.scalar.copy(b_sb[t][:], b_ps[t][:])
+        for t in range(PACK - 1):
+            nc.vector.tensor_copy(g4[t][:], b_sb[t][:].indirect(n4_t[:]))
+
+        out_rows = out_0.rearrange("(p t) c -> p t c", t=PACK)
+        o_pl = sb("o_pl", [P, PACK, S], BF16)
+        a_sb = [sb(f"a{t}", [P, S], F32) for t in range(PACK)]
+        g3 = [sb(f"g3_{t}", [P, W], F32) for t in range(PACK)]
+        for t in range(PACK):
+            nc.scalar.activation(a_sb[t][:], a_ps[t][:], COPY, scale=0.0625)
+            nc.scalar.activation(g3[t][:], a_sb[t][:].indirect(n3_t[:]), COPY, scale=-0.5)
+        nc.scalar.activation(g4[3][:], b_sb[3][:].indirect(n4_t[:]), COPY)
+        for t in range(PACK):
+            nc.vector.tensor_tensor(a_sb[t][:].indirect(n3_t[:]), g3[t][:], g4[t][:], ALU.add)
+            nc.sync.dma_start(out_rows[:, t, :], a_sb[t][:])
+        for t in range(PACK - 1):
+            nc.scalar.copy(o_pl[:, t, :], a_sb[t][:])
+        nc.vector.tensor_copy(o_pl[:, 3, :], a_sb[3][:])
+
+        o_il = sb("o_il", [P, S, PACK], BF16)
+        interleave(nc.vector.tensor_copy, o_il, o_pl, 0, 384)
+        interleave(nc.scalar.copy, o_il, o_pl, 384, S)
+        o_c, o_s = quantize("o", o_il)
+        nc.sync.dma_start(out_1[0].rearrange("p n t -> p (n t)").bitcast(I32), o_c[:])
+        for q in range(4):
+            nc.scalar.dma_start(out_2[0, 4 * q : 4 * q + 4, :].bitcast(I32), o_s[32 * q : 32 * q + 4, :].bitcast(I32))

@@ -11,7 +11,8 @@ U8 = mybir.dt.uint8
 FP8X4 = mybir.dt.float8_e4m3fn_x4
 FP4X4 = mybir.dt.float4_e2m1fn_x4
 ALU = mybir.AluOpType
-COPY = mybir.ActivationFunctionType.Copy
+ACT = mybir.ActivationFunctionType
+COPY = ACT.Copy
 
 P = 128
 PACK = 4
@@ -19,6 +20,9 @@ T = 2048
 S = 512
 W = 256
 SPARE = 16
+SPLIT = 352
+CLEAR = 1280
+FIRST = 512
 FLOPS = 3 * 2 * 512 * 512 * 512
 
 
@@ -31,8 +35,8 @@ def tile_picked_cdswputbhopmn_none_po_kernel(
         keep = ctx.enter_context(tc.tile_pool(name="keep", bufs=1))
         psum = ctx.enter_context(tc.psum_pool(name="psum", bufs=1))
 
-        def sb(name, shape, dtype):
-            return keep.tile(shape, dtype, name=name, align_bytes=64)
+        def sb(name, shape, dtype, tag=None):
+            return keep.tile(shape, dtype, name=name, tag=tag or name, align_bytes=64)
 
         def load_list(name, src):
             tile = lists.tile(list(src.shape), U16, name=name)
@@ -45,53 +49,49 @@ def tile_picked_cdswputbhopmn_none_po_kernel(
 
         x_s = sb("x_s", [P, T], U8)
         w1_s = sb("w1_s", [P, S], U8)
-        nc.vector.memset(x_s[:].bitcast(I32), 0)
-        nc.gpsimd.memset(w1_s[:].bitcast(I32), 0)
-        x_w = sb("x_w", [P, T], I32)
-        x_src = x_words[0].rearrange("p n t -> p (n t)").bitcast(I32)
-        nc.sync.dma_start(x_w[:, : T // 2], x_src[:, : T // 2])
-        load_scale_rows(x_s, x_scales)
-        offs_t = load_list("offs_t", offs)
+        nc.vector.memset(x_s[:, :CLEAR].bitcast(I32), 0)
+        nc.gpsimd.memset(x_s[:, CLEAR:].bitcast(I32), 0)
+        nc.vector.memset(w1_s[:].bitcast(I32), 0)
         w1_w = sb("w1_w", [P, 2 * S], U8)
         nc.sync.dma_start(w1_w[:].bitcast(I32), w1_words[0].bitcast(I32))
-        nc.sync.dma_start(x_w[:, T // 2 :], x_src[:, T // 2 :])
+        offs_t = load_list("offs_t", offs)
+        x_w = sb("x_w", [P, T], I32)
+        x_src = x_words[0].rearrange("p n t -> p (n t)").bitcast(I32)
+        nc.sync.dma_start(x_w[:, :FIRST], x_src[:, :FIRST])
+        load_scale_rows(x_s, x_scales)
+        nc.sync.dma_start(x_w[:, FIRST:], x_src[:, FIRST:])
         load_scale_rows(w1_s, w1_scales)
-        cand_t = load_list("cand_t", cand)
-        cb_t = load_list("cb_t", cb)
-        n1_t = load_list("n1_t", n1)
-        wb_raw = sb("wb_raw", [P, PACK, S], F32)
-        nc.sync.dma_start(wb_raw[:], wb.rearrange("(p j) c -> p j c", j=PACK))
-        n2_t = load_list("n2_t", n2)
         gs_t = sb("gs_t", [P, PACK], F32)
         nc.sync.dma_start(gs_t[:], gs.rearrange("(p j) o -> p (j o)", j=PACK))
+        cand_t = load_list("cand_t", cand)
+        n1_t = load_list("n1_t", n1)
+        cb_t = load_list("cb_t", cb)
+        n2_t = load_list("n2_t", n2)
+        wb_raw = sb("wb_raw", [P, PACK, S], F32)
+        nc.sync.dma_start(wb_raw[:], wb.rearrange("(p j) c -> p j c", j=PACK))
         n4_t = load_list("n4_t", n4)
         n3_t = load_list("n3_t", n3)
 
-        y_sb = [sb(f"y{t}", [P, S + SPARE], F32) for t in range(PACK)]
-        st_sb = [sb(f"st{t}", [P, S + SPARE], F32) for t in range(PACK)]
-        for t in range(PACK):
-            nc.gpsimd.memset(y_sb[t][:, S:], 0.0)
-            nc.gpsimd.memset(st_sb[t][:, S:], 0.0)
+        gs_abs = sb("gs_abs", [P, PACK], F32)
+        gs_sign = sb("gs_sign", [P, PACK], F32)
+        nc.scalar.activation(gs_abs[:], gs_t[:], ACT.Abs)
+        nc.scalar.activation(gs_sign[:], gs_t[:], ACT.Sign)
 
-        xq_s = sb("xq_s", [P, S], U8)
-        nc.vector.tensor_copy(xq_s[:], x_s[:].indirect(offs_t[:]))
+        y_sb = [sb(f"y{t}", [P, S + SPARE], F32) for t in range(PACK)]
+        st_sb = [sb(f"st{t}", [P, S + SPARE if t in (1, 2) else S], F32) for t in range(PACK)]
+        for tile in y_sb + st_sb[1:3]:
+            nc.gpsimd.memset(tile[:, S:], 0.0)
+
         w1_wd = sb("w1_wd", [P, 2 * S], U8)
         nc.vector.tensor_copy(
             w1_wd[:].rearrange("p (t m e) -> p t m e", t=PACK, e=2), w1_w[:].rearrange("p (m t e) -> p t m e", t=PACK, e=2)
         )
+        xq_s = sb("xq_s", [P, S], U8, "w1_w")
+        nc.vector.tensor_copy(xq_s[:], x_s[:].indirect(offs_t[:]))
         w1_sd = sb("w1_sd", [P, S], U8)
         nc.vector.tensor_copy(w1_sd[:].rearrange("p (t m) -> p t m", t=PACK), w1_s[:].rearrange("p (m t) -> p t m", t=PACK))
         xq_w = sb("xq_w", [P, S], U32)
         nc.vector.tensor_copy(xq_w[:], x_w[:].bitcast(U32).indirect(offs_t[:]))
-
-        def dealt_columns(name, picks):
-            words = sb(name + "_w", [P, S], U32)
-            nc.vector.tensor_copy(words[:].rearrange("p (t m) -> p m t", t=PACK), x_w[:].bitcast(U32).indirect(picks[:]))
-            raw = sb(name + "_raw", [P, S], U8)
-            nc.vector.tensor_copy(raw[:], x_s[:].indirect(picks[:]))
-            scales = sb(name + "_s", [P, S], U8)
-            nc.vector.tensor_copy(scales[:].rearrange("p (t m) -> p t m", t=PACK), raw[:].rearrange("p (m t) -> p t m", t=PACK))
-            return words, scales
 
         def interleave(engine_copy, dst, src, c0, c1):
             engine_copy(
@@ -99,8 +99,8 @@ def tile_picked_cdswputbhopmn_none_po_kernel(
                 src[:, :, c0:c1].rearrange("p t (c i) -> p c t i", i=4),
             )
 
-        def quantize(name, grouped):
-            codes = sb(name + "_codes", [P, S], I32)
+        def quantize(name, grouped, tag=None):
+            codes = sb(name + "_codes", [P, S], I32, tag)
             scales = sb(name + "_scales", [P, S], U8)
             nc.vector.quantize_mx(out=codes[:].bitcast(FP8X4), scales=scales[:], in_=grouped[:].rearrange("p c t -> p (c t)"))
             return codes, scales
@@ -108,8 +108,8 @@ def tile_picked_cdswputbhopmn_none_po_kernel(
         def product(bank, t, words, scales, codes, code_scales):
             cols = slice(t * P, (t + 1) * P)
             nc.tensor.matmul_mx(
-                out=bank[:], lhsT=words[:, cols].bitcast(FP8X4), lhsT_scale=scales[:, cols],
-                rhs=codes[:].bitcast(FP8X4), rhs_scale=code_scales[:], start=True, stop=True,
+                out=bank, lhsT=words[:, cols].bitcast(FP8X4), lhsT_scale=scales[:, cols],
+                rhs=codes.bitcast(FP8X4), rhs_scale=code_scales, start=True, stop=True,
             )
 
         y_ps = [psum.tile([P, S], F32, name=f"y_ps{t}", tag=f"ya{t}") for t in range(PACK)]
@@ -119,66 +119,109 @@ def tile_picked_cdswputbhopmn_none_po_kernel(
                 rhs=xq_w[:].bitcast(FP8X4), rhs_scale=xq_s[:], start=True, stop=True,
             )
 
-        cand_w, cand_s = dealt_columns("cand", cand_t)
-        cb_w, cb_s = dealt_columns("cb", cb_t)
+        picked_raw = sb("picked_raw", [P, 2, S], U8)
+        picked_s = sb("picked_s", [P, 2, S], U8)
+        picked_w = [sb(f"picked_w{i}", [P, S], U32) for i in range(2)]
+        for i, picks in enumerate((cand_t, cb_t)):
+            nc.vector.tensor_copy(picked_raw[:, i, :], x_s[:].indirect(picks[:]))
+            nc.vector.tensor_copy(picked_w[i][:].rearrange("p (t m) -> p m t", t=PACK), x_w[:].bitcast(U32).indirect(picks[:]))
+        nc.vector.tensor_copy(
+            picked_s[:].rearrange("p l (t m) -> p l t m", t=PACK), picked_raw[:].rearrange("p l (m t) -> p l t m", t=PACK)
+        )
+        cand_w, cb_w = picked_w
+        cand_s, cb_s = picked_s[:, 0, :], picked_s[:, 1, :]
 
         g1 = [sb(f"g1_{t}", [P, S], F32) for t in range(PACK)]
         for t in range(PACK):
-            nc.scalar.copy(y_sb[t][:, :S], y_ps[t][:])
+            nc.scalar.activation(y_sb[t][:, :S], y_ps[t][:], COPY, scale=gs_abs[:, t : t + 1])
             nc.scalar.activation(g1[t][:], y_sb[t][:].indirect(n1_t[:]), COPY)
-        for t in range(PACK):
-            nc.vector.tensor_tensor(st_sb[t][:, :S], y_sb[t][:, :S], g1[t][:], ALU.max)
+        g2 = [sb(f"g2_{t}", [P, S], F32) for t in range(PACK)]
+        z_pl = sb("z_pl", [P, PACK, S], BF16)
+        mn = [sb(f"mn_{t}", [P, S], BF16) for t in range(PACK)]
+        halves = [slice(0, W), slice(W, S)]
+        list_halves = [slice(0, W // 16), slice(W // 16, S // 16)]
+
+        def larger(t):
+            nc.vector.scalar_tensor_tensor(st_sb[t][:, :S], y_ps[t][:], gs_abs[:, t : t + 1], g1[t][:], ALU.mult, ALU.max)
+
+        def smaller(t, cols):
+            nc.vector.tensor_tensor(mn[t][:, cols], st_sb[t][:, cols], g2[t][:, cols], ALU.min)
+
+        def signed(t, cols):
+            nc.vector.tensor_scalar(z_pl[:, t, cols], mn[t][:, cols], gs_sign[:, t : t + 1], None, ALU.mult)
+
+        whole = slice(0, S)
+        larger(0)
+        for h in range(2):
+            nc.vector.tensor_copy(g2[0][:, halves[h]], st_sb[0][:].indirect(n2_t[:, list_halves[h]]))
+        for t in range(1, PACK):
+            larger(t)
+        for t in (1, 2):
+            nc.scalar.activation(g2[t][:], st_sb[t][:].indirect(n2_t[:]), COPY)
+        for h in range(2):
+            nc.scalar.activation(g2[3][:, halves[h]], st_sb[3][:].indirect(n2_t[:, list_halves[h]]), COPY)
 
         wb_il = sb("wb_il", [P, S, PACK], BF16)
         interleave(nc.vector.tensor_copy, wb_il, wb_raw, 0, S)
         wb_c, wb_s = quantize("wb", wb_il)
-        b_ps = [psum.tile([P, S], F32, name=f"b_ps{t}") for t in range(PACK)]
+        b_ps = [psum.tile([P, S], F32, name=f"b_ps{t}", tag=f"b{t}") for t in range(PACK)]
         for t in range(PACK):
-            product(b_ps[t], t, cb_w, cb_s, wb_c, wb_s)
+            product(b_ps[t][:], t, cb_w, cb_s, wb_c[:], wb_s[:])
 
-        g2 = [sb(f"g2_{t}", [P, S], F32) for t in range(PACK)]
         for t in range(PACK - 1):
-            nc.scalar.activation(g2[t][:], st_sb[t][:].indirect(n2_t[:]), COPY)
-        for h in range(2):
-            nc.vector.tensor_copy(g2[3][:, h * W : (h + 1) * W], st_sb[3][:].indirect(n2_t[:, 16 * h : 16 * (h + 1)]))
-        z_pl = sb("z_pl", [P, PACK, S], BF16)
-        mn = [sb(f"mn_{t}", [P, S], F32) for t in range(PACK)]
-        for t in (0, 3, 1, 2):
-            nc.vector.tensor_tensor(mn[t][:], st_sb[t][:, :S], g2[t][:], ALU.min)
-            nc.vector.tensor_scalar(z_pl[:, t, :], mn[t][:], gs_t[:, t : t + 1], None, ALU.mult)
-
+            smaller(t, whole)
+            signed(t, whole)
         z_il = sb("z_il", [P, S, PACK], BF16)
-        interleave(nc.vector.tensor_copy, z_il, z_pl, 0, S)
-        z_c, z_s = quantize("z", z_il)
-        a_ps = [psum.tile([P, S], F32, name=f"a_ps{t}", tag=f"ya{t}") for t in range(PACK)]
-        for t in range(PACK):
-            product(a_ps[t], t, cand_w, cand_s, z_c, z_s)
+        z_c = sb("z_codes", [P, S], I32)
+        z_s = sb("z_scales", [P, S], U8)
+        for cols in halves:
+            smaller(3, cols)
+            signed(3, cols)
+            interleave(nc.vector.tensor_copy, z_il, z_pl, cols.start, cols.stop)
+            nc.vector.quantize_mx(
+                out=z_c[:, cols].bitcast(FP8X4), scales=z_s[:, cols], in_=z_il[:, cols, :].rearrange("p c t -> p (c t)")
+            )
 
         b_sb = [sb(f"b{t}", [P, S], F32) for t in range(PACK)]
-        g4 = [sb(f"g4_{t}", [P, W], F32) for t in range(PACK)]
-        for t in range(PACK):
-            nc.scalar.copy(b_sb[t][:], b_ps[t][:])
-        for t in range(PACK - 1):
-            nc.vector.tensor_copy(g4[t][:], b_sb[t][:].indirect(n4_t[:]))
+        g4_early = sb("g4_early", [P, 2, W], F32, "z_il")
+        g4_late = {2: "z_pl", 3: "g3_0"}
+        g4 = [g4_early[:, t, :] for t in range(2)]
+        nc.scalar.copy(b_sb[0][:], b_ps[0][:])
+        a_ps = [psum.tile([P, S], F32, name=f"a_ps{t}", tag=f"ya{t}") for t in range(PACK)]
+        a0_tail = psum.tile([P, W], F32, name="a0_tail", tag="b0")
+        a_half = [[a_ps[t][:, cols] for cols in halves] for t in range(PACK)]
+        a_half[0][1] = a0_tail[:]
+        for h, cols in enumerate(halves):
+            for t in range(PACK):
+                product(a_half[t][h], t, cand_w, cand_s, z_c[:, cols], z_s[:, cols])
 
         out_rows = out_0.rearrange("(p t) c -> p t c", t=PACK)
         o_pl = sb("o_pl", [P, PACK, S], BF16)
         a_sb = [sb(f"a{t}", [P, S], F32) for t in range(PACK)]
         g3 = [sb(f"g3_{t}", [P, W], F32) for t in range(PACK)]
+        nc.scalar.activation(a_sb[0][:, halves[0]], a_half[0][0], COPY, scale=0.0625)
+        nc.vector.tensor_scalar(a_sb[0][:, halves[1]], a_half[0][1], 0.0625, None, ALU.mult)
+        nc.vector.tensor_scalar(g3[0][:], a_sb[0][:].indirect(n3_t[:]), -0.5, 0.0, ALU.mult, ALU.add)
+        for t in range(1, PACK):
+            nc.scalar.copy(b_sb[t][:], b_ps[t][:])
+        for t in range(2):
+            nc.vector.tensor_copy(g4[t], b_sb[t][:].indirect(n4_t[:]))
         for t in range(PACK):
-            nc.scalar.activation(a_sb[t][:], a_ps[t][:], COPY, scale=0.0625)
-            nc.scalar.activation(g3[t][:], a_sb[t][:].indirect(n3_t[:]), COPY, scale=-0.5)
-        nc.scalar.activation(g4[3][:], b_sb[3][:].indirect(n4_t[:]), COPY)
-        for t in range(PACK):
-            nc.vector.tensor_tensor(a_sb[t][:].indirect(n3_t[:]), g3[t][:], g4[t][:], ALU.add)
+            if t > 0:
+                nc.scalar.activation(a_sb[t][:], a_ps[t][:], COPY, scale=0.0625)
+                nc.scalar.activation(g3[t][:], a_sb[t][:].indirect(n3_t[:]), COPY, scale=-0.5)
+            if t in g4_late:
+                g4.append(sb(f"g4_{t}", [P, W], F32, g4_late[t])[:])
+                nc.scalar.activation(g4[t], b_sb[t][:].indirect(n4_t[:]), COPY)
+            nc.vector.tensor_tensor(a_sb[t][:].indirect(n3_t[:]), g3[t][:], g4[t], ALU.add)
             nc.sync.dma_start(out_rows[:, t, :], a_sb[t][:])
         for t in range(PACK - 1):
             nc.scalar.copy(o_pl[:, t, :], a_sb[t][:])
-        nc.vector.tensor_copy(o_pl[:, 3, :], a_sb[3][:])
 
         o_il = sb("o_il", [P, S, PACK], BF16)
-        interleave(nc.vector.tensor_copy, o_il, o_pl, 0, 384)
-        interleave(nc.scalar.copy, o_il, o_pl, 384, S)
+        for copy, c0, c1 in ((nc.vector.tensor_copy, 0, SPLIT), (nc.scalar.copy, SPLIT, S)):
+            copy(o_pl[:, 3, c0:c1], a_sb[3][:, c0:c1])
+            interleave(copy, o_il, o_pl, c0, c1)
         o_c, o_s = quantize("o", o_il)
         nc.sync.dma_start(out_1[0].rearrange("p n t -> p (n t)").bitcast(I32), o_c[:])
         for q in range(4):

@@ -78,8 +78,8 @@ def tile_picked_cdswputbhopmn_none_po_kernel(
         nc.scalar.activation(gs_sign[:], gs_t[:], ACT.Sign)
 
         y_sb = [sb(f"y{t}", [P, S + SPARE], F32) for t in range(PACK)]
-        st_sb = [sb(f"st{t}", [P, S + SPARE if t in (1, 2) else S], F32) for t in range(PACK)]
-        for tile in y_sb + st_sb[1:3]:
+        st_sb = [sb(f"st{t}", [P, S + SPARE if t == 2 else S], F32) for t in range(PACK)]
+        for tile in y_sb + st_sb[2:3]:
             nc.gpsimd.memset(tile[:, S:], 0.0)
 
         w1_wd = sb("w1_wd", [P, 2 * S], U8)
@@ -137,7 +137,6 @@ def tile_picked_cdswputbhopmn_none_po_kernel(
             nc.scalar.activation(g1[t][:], y_sb[t][:].indirect(n1_t[:]), COPY)
         g2 = [sb(f"g2_{t}", [P, S], F32) for t in range(PACK)]
         z_pl = sb("z_pl", [P, PACK, S], BF16)
-        mn = [sb(f"mn_{t}", [P, S], BF16) for t in range(PACK)]
         halves = [slice(0, W), slice(W, S)]
         list_halves = [slice(0, W // 16), slice(W // 16, S // 16)]
 
@@ -145,25 +144,29 @@ def tile_picked_cdswputbhopmn_none_po_kernel(
             nc.vector.scalar_tensor_tensor(st_sb[t][:, :S], y_ps[t][:], gs_abs[:, t : t + 1], g1[t][:], ALU.mult, ALU.max)
 
         def smaller(t, cols):
-            nc.vector.tensor_tensor(mn[t][:, cols], st_sb[t][:, cols], g2[t][:, cols], ALU.min)
+            nc.vector.tensor_tensor(mn[t // 2][:, t % 2, cols], st_sb[t][:, cols], g2[t][:, cols], ALU.min)
 
         def signed(t, cols):
-            nc.vector.tensor_scalar(z_pl[:, t, cols], mn[t][:, cols], gs_sign[:, t : t + 1], None, ALU.mult)
+            nc.vector.tensor_scalar(z_pl[:, t, cols], mn[t // 2][:, t % 2, cols], gs_sign[:, t : t + 1], None, ALU.mult)
 
         whole = slice(0, S)
         larger(0)
         for h in range(2):
             nc.vector.tensor_copy(g2[0][:, halves[h]], st_sb[0][:].indirect(n2_t[:, list_halves[h]]))
-        for t in range(1, PACK):
-            larger(t)
-        for t in (1, 2):
-            nc.scalar.activation(g2[t][:], st_sb[t][:].indirect(n2_t[:]), COPY)
+        larger(1)
+        nc.vector.tensor_copy(g2[1][:, halves[0]], st_sb[1][:].indirect(n2_t[:, list_halves[0]]))
+        larger(2)
+        larger(3)
+        nc.scalar.activation(g2[1][:, halves[1]], st_sb[1][:].indirect(n2_t[:, list_halves[1]]), COPY)
+        nc.scalar.activation(g2[2][:], st_sb[2][:].indirect(n2_t[:]), COPY)
         for h in range(2):
             nc.scalar.activation(g2[3][:, halves[h]], st_sb[3][:].indirect(n2_t[:, list_halves[h]]), COPY)
 
         wb_il = sb("wb_il", [P, S, PACK], BF16)
-        interleave(nc.vector.tensor_copy, wb_il, wb_raw, 0, S)
+        for c0 in range(0, S, P):
+            interleave(lambda o, i: nc.gpsimd.tensor_scalar(o, i, 1.0, 0.0, ALU.mult, ALU.add), wb_il, wb_raw, c0, c0 + P)
         wb_c, wb_s = quantize("wb", wb_il)
+        mn = [sb("mn_early", [P, 2, S], BF16), sb("mn_late", [P, 2, S], BF16, "wb_il")]
         b_ps = [psum.tile([P, S], F32, name=f"b_ps{t}", tag=f"b{t}") for t in range(PACK)]
         for t in range(PACK):
             product(b_ps[t][:], t, cb_w, cb_s, wb_c[:], wb_s[:])
@@ -184,7 +187,7 @@ def tile_picked_cdswputbhopmn_none_po_kernel(
 
         b_sb = [sb(f"b{t}", [P, S], F32) for t in range(PACK)]
         g4_early = sb("g4_early", [P, 2, W], F32, "z_il")
-        g4_late = {2: "z_pl", 3: "g3_0"}
+        g4_late = {2: "g3_0", 3: "g3_1"}
         g4 = [g4_early[:, t, :] for t in range(2)]
         nc.scalar.copy(b_sb[0][:], b_ps[0][:])
         a_ps = [psum.tile([P, S], F32, name=f"a_ps{t}", tag=f"ya{t}") for t in range(PACK)]
@@ -199,8 +202,8 @@ def tile_picked_cdswputbhopmn_none_po_kernel(
         o_pl = sb("o_pl", [P, PACK, S], BF16)
         a_sb = [sb(f"a{t}", [P, S], F32) for t in range(PACK)]
         g3 = [sb(f"g3_{t}", [P, W], F32) for t in range(PACK)]
-        nc.scalar.activation(a_sb[0][:, halves[0]], a_half[0][0], COPY, scale=0.0625)
-        nc.vector.tensor_scalar(a_sb[0][:, halves[1]], a_half[0][1], 0.0625, None, ALU.mult)
+        for h, cols in enumerate(halves):
+            nc.scalar.activation(a_sb[0][:, cols], a_half[0][h], COPY, scale=0.0625)
         nc.vector.tensor_scalar(g3[0][:], a_sb[0][:].indirect(n3_t[:]), -0.5, 0.0, ALU.mult, ALU.add)
         for t in range(1, PACK):
             nc.scalar.copy(b_sb[t][:], b_ps[t][:])
@@ -225,4 +228,4 @@ def tile_picked_cdswputbhopmn_none_po_kernel(
         o_c, o_s = quantize("o", o_il)
         nc.sync.dma_start(out_1[0].rearrange("p n t -> p (n t)").bitcast(I32), o_c[:])
         for q in range(4):
-            nc.scalar.dma_start(out_2[0, 4 * q : 4 * q + 4, :].bitcast(I32), o_s[32 * q : 32 * q + 4, :].bitcast(I32))
+            (nc.scalar if q < 2 else nc.sync).dma_start(out_2[0, 4 * q : 4 * q + 4, :].bitcast(I32), o_s[32 * q : 32 * q + 4, :].bitcast(I32))

from contextlib import ExitStack

import concourse.mybir as mybir

F32 = mybir.dt.float32
BF16 = mybir.dt.bfloat16
I32 = mybir.dt.int32
U32 = mybir.dt.uint32
U16 = mybir.dt.uint16
U8 = mybir.dt.uint8
FP8X4 = mybir.dt.float8_e4m3fn_x4
FP4X4 = mybir.dt.float4_e2m1fn_x4
ALU = mybir.AluOpType
ACT = mybir.ActivationFunctionType
COPY = ACT.Copy

P = 128
PACK = 4
T = 2048
S = 512
W = 256
SPARE = 16
SPLIT = 352
CLEAR = 1280
FIRST = 512
FLOPS = 3 * 2 * 512 * 512 * 512


def tile_picked_cdswputbhopmn_none_po_kernel(
    tc, x_words, x_scales, w1_words, w1_scales, gs, wb, offs, n1, n2, cand, cb, n3, n4, out_0, out_1, out_2
):
    nc = tc.nc
    with ExitStack() as ctx:
        lists = ctx.enter_context(tc.tile_pool(name="lists", bufs=1))
        keep = ctx.enter_context(tc.tile_pool(name="keep", bufs=1))
        psum = ctx.enter_context(tc.psum_pool(name="psum", bufs=1))

        def sb(name, shape, dtype, tag=None):
            return keep.tile(shape, dtype, name=name, tag=tag or name, align_bytes=64)

        def load_list(name, src):
            tile = lists.tile(list(src.shape), U16, name=name)
            nc.sync.dma_start(tile[:], src)
            return tile

        def load_scale_rows(tile, src):
            for q in range(4):
                nc.sync.dma_start(tile[32 * q : 32 * q + 4, :].bitcast(I32), src[0, 4 * q : 4 * q + 4, :].bitcast(I32))

        x_s = sb("x_s", [P, T], U8)
        w1_s = sb("w1_s", [P, S], U8)
        nc.vector.memset(x_s[:, :CLEAR].bitcast(I32), 0)
        nc.gpsimd.memset(x_s[:, CLEAR:].bitcast(I32), 0)
        nc.vector.memset(w1_s[:].bitcast(I32), 0)
        w1_w = sb("w1_w", [P, 2 * S], U8)
        nc.sync.dma_start(w1_w[:].bitcast(I32), w1_words[0].bitcast(I32))
        offs_t = load_list("offs_t", offs)
        x_w = sb("x_w", [P, T], I32)
        x_src = x_words[0].rearrange("p n t -> p (n t)").bitcast(I32)
        nc.sync.dma_start(x_w[:, :FIRST], x_src[:, :FIRST])
        load_scale_rows(x_s, x_scales)
        nc.sync.dma_start(x_w[:, FIRST:], x_src[:, FIRST:])
        load_scale_rows(w1_s, w1_scales)
        gs_t = sb("gs_t", [P, PACK], F32)
        nc.sync.dma_start(gs_t[:], gs.rearrange("(p j) o -> p (j o)", j=PACK))
        cand_t = load_list("cand_t", cand)
        n1_t = load_list("n1_t", n1)
        cb_t = load_list("cb_t", cb)
        n2_t = load_list("n2_t", n2)
        wb_raw = sb("wb_raw", [P, PACK, S], F32)
        nc.sync.dma_start(wb_raw[:], wb.rearrange("(p j) c -> p j c", j=PACK))
        n4_t = load_list("n4_t", n4)
        n3_t = load_list("n3_t", n3)

        gs_abs = sb("gs_abs", [P, PACK], F32)
        gs_sign = sb("gs_sign", [P, PACK], F32)
        nc.scalar.activation(gs_abs[:], gs_t[:], ACT.Abs)
        nc.scalar.activation(gs_sign[:], gs_t[:], ACT.Sign)

        y_sb = [sb(f"y{t}", [P, S + SPARE], F32) for t in range(PACK)]
        st_sb = [sb(f"st{t}", [P, S + SPARE if t == 2 else S], F32) for t in range(PACK)]
        for tile in y_sb + st_sb[2:3]:
            nc.gpsimd.memset(tile[:, S:], 0.0)

        w1_wd = sb("w1_wd", [P, 2 * S], U8)
        nc.vector.tensor_copy(
            w1_wd[:].rearrange("p (t m e) -> p t m e", t=PACK, e=2), w1_w[:].rearrange("p (m t e) -> p t m e", t=PACK, e=2)
        )
        xq_s = sb("xq_s", [P, S], U8, "w1_w")
        nc.vector.tensor_copy(xq_s[:], x_s[:].indirect(offs_t[:]))
        w1_sd = sb("w1_sd", [P, S], U8)
        nc.vector.tensor_copy(w1_sd[:].rearrange("p (t m) -> p t m", t=PACK), w1_s[:].rearrange("p (m t) -> p t m", t=PACK))
        xq_w = sb("xq_w", [P, S], U32)
        nc.vector.tensor_copy(xq_w[:], x_w[:].bitcast(U32).indirect(offs_t[:]))

        def interleave(engine_copy, dst, src, c0, c1):
            engine_copy(
                dst[:, c0:c1, :].rearrange("p (c i) t -> p c t i", i=4),
                src[:, :, c0:c1].rearrange("p t (c i) -> p c t i", i=4),
            )

        def quantize(name, grouped, tag=None):
            codes = sb(name + "_codes", [P, S], I32, tag)
            scales = sb(name + "_scales", [P, S], U8)
            nc.vector.quantize_mx(out=codes[:].bitcast(FP8X4), scales=scales[:], in_=grouped[:].rearrange("p c t -> p (c t)"))
            return codes, scales

        def product(bank, t, words, scales, codes, code_scales):
            cols = slice(t * P, (t + 1) * P)
            nc.tensor.matmul_mx(
                out=bank, lhsT=words[:, cols].bitcast(FP8X4), lhsT_scale=scales[:, cols],
                rhs=codes.bitcast(FP8X4), rhs_scale=code_scales, start=True, stop=True,
            )

        y_ps = [psum.tile([P, S], F32, name=f"y_ps{t}", tag=f"ya{t}") for t in range(PACK)]
        for t in range(PACK):
            nc.tensor.matmul_mx(
                out=y_ps[t][:], lhsT=w1_wd[:, 2 * P * t : 2 * P * (t + 1)].bitcast(FP4X4), lhsT_scale=w1_sd[:, P * t : P * (t + 1)],
                rhs=xq_w[:].bitcast(FP8X4), rhs_scale=xq_s[:], start=True, stop=True,
            )

        picked_raw = sb("picked_raw", [P, 2, S], U8)
        picked_s = sb("picked_s", [P, 2, S], U8)
        picked_w = [sb(f"picked_w{i}", [P, S], U32) for i in range(2)]
        for i, picks in enumerate((cand_t, cb_t)):
            nc.vector.tensor_copy(picked_raw[:, i, :], x_s[:].indirect(picks[:]))
            nc.vector.tensor_copy(picked_w[i][:].rearrange("p (t m) -> p m t", t=PACK), x_w[:].bitcast(U32).indirect(picks[:]))
        nc.vector.tensor_copy(
            picked_s[:].rearrange("p l (t m) -> p l t m", t=PACK), picked_raw[:].rearrange("p l (m t) -> p l t m", t=PACK)
        )
        cand_w, cb_w = picked_w
        cand_s, cb_s = picked_s[:, 0, :], picked_s[:, 1, :]

        g1 = [sb(f"g1_{t}", [P, S], F32) for t in range(PACK)]
        for t in range(PACK):
            nc.scalar.activation(y_sb[t][:, :S], y_ps[t][:], COPY, scale=gs_abs[:, t : t + 1])
            nc.scalar.activation(g1[t][:], y_sb[t][:].indirect(n1_t[:]), COPY)
        g2 = [sb(f"g2_{t}", [P, S], F32) for t in range(PACK)]
        z_pl = sb("z_pl", [P, PACK, S], BF16)
        halves = [slice(0, W), slice(W, S)]
        list_halves = [slice(0, W // 16), slice(W // 16, S // 16)]

        def larger(t):
            nc.vector.scalar_tensor_tensor(st_sb[t][:, :S], y_ps[t][:], gs_abs[:, t : t + 1], g1[t][:], ALU.mult, ALU.max)

        def smaller(t, cols):
            nc.vector.tensor_tensor(mn[t // 2][:, t % 2, cols], st_sb[t][:, cols], g2[t][:, cols], ALU.min)

        def signed(t, cols):
            nc.vector.tensor_scalar(z_pl[:, t, cols], mn[t // 2][:, t % 2, cols], gs_sign[:, t : t + 1], None, ALU.mult)

        whole = slice(0, S)
        larger(0)
        for h in range(2):
            nc.vector.tensor_copy(g2[0][:, halves[h]], st_sb[0][:].indirect(n2_t[:, list_halves[h]]))
        larger(1)
        nc.vector.tensor_copy(g2[1][:, halves[0]], st_sb[1][:].indirect(n2_t[:, list_halves[0]]))
        larger(2)
        larger(3)
        nc.scalar.activation(g2[1][:, halves[1]], st_sb[1][:].indirect(n2_t[:, list_halves[1]]), COPY)
        nc.scalar.activation(g2[2][:], st_sb[2][:].indirect(n2_t[:]), COPY)
        for h in range(2):
            nc.scalar.activation(g2[3][:, halves[h]], st_sb[3][:].indirect(n2_t[:, list_halves[h]]), COPY)

        wb_il = sb("wb_il", [P, S, PACK], BF16)
        for c0 in range(0, S, P):
            interleave(lambda o, i: nc.gpsimd.tensor_scalar(o, i, 1.0, 0.0, ALU.mult, ALU.add), wb_il, wb_raw, c0, c0 + P)
        wb_c, wb_s = quantize("wb", wb_il)
        mn = [sb("mn_early", [P, 2, S], BF16), sb("mn_late", [P, 2, S], BF16, "wb_il")]
        b_ps = [psum.tile([P, S], F32, name=f"b_ps{t}", tag=f"b{t}") for t in range(PACK)]
        for t in range(PACK):
            product(b_ps[t][:], t, cb_w, cb_s, wb_c[:], wb_s[:])

        for t in range(PACK - 1):
            smaller(t, whole)
            signed(t, whole)
        z_il = sb("z_il", [P, S, PACK], BF16)
        z_c = sb("z_codes", [P, S], I32)
        z_s = sb("z_scales", [P, S], U8)
        for cols in halves:
            smaller(3, cols)
            signed(3, cols)
            interleave(nc.vector.tensor_copy, z_il, z_pl, cols.start, cols.stop)
            nc.vector.quantize_mx(
                out=z_c[:, cols].bitcast(FP8X4), scales=z_s[:, cols], in_=z_il[:, cols, :].rearrange("p c t -> p (c t)")
            )

        b_sb = [sb(f"b{t}", [P, S], F32) for t in range(PACK)]
        g4_early = sb("g4_early", [P, 2, W], F32, "z_il")
        g4_late = {2: "g3_0", 3: "g3_1"}
        g4 = [g4_early[:, t, :] for t in range(2)]
        nc.scalar.copy(b_sb[0][:], b_ps[0][:])
        a_ps = [psum.tile([P, S], F32, name=f"a_ps{t}", tag=f"ya{t}") for t in range(PACK)]
        a0_tail = psum.tile([P, W], F32, name="a0_tail", tag="b0")
        a_half = [[a_ps[t][:, cols] for cols in halves] for t in range(PACK)]
        a_half[0][1] = a0_tail[:]
        for h, cols in enumerate(halves):
            for t in range(PACK):
                product(a_half[t][h], t, cand_w, cand_s, z_c[:, cols], z_s[:, cols])

        out_rows = out_0.rearrange("(p t) c -> p t c", t=PACK)
        o_pl = sb("o_pl", [P, PACK, S], BF16)
        a_sb = [sb(f"a{t}", [P, S], F32) for t in range(PACK)]
        g3 = [sb(f"g3_{t}", [P, W], F32) for t in range(PACK)]
        for h, cols in enumerate(halves):
            nc.scalar.activation(a_sb[0][:, cols], a_half[0][h], COPY, scale=0.0625)
        nc.vector.tensor_scalar(g3[0][:], a_sb[0][:].indirect(n3_t[:]), -0.5, 0.0, ALU.mult, ALU.add)
        for t in range(1, PACK):
            nc.scalar.copy(b_sb[t][:], b_ps[t][:])
        for t in range(2):
            nc.vector.tensor_copy(g4[t], b_sb[t][:].indirect(n4_t[:]))
        for t in range(PACK):
            if t > 0:
                nc.scalar.activation(a_sb[t][:], a_ps[t][:], COPY, scale=0.0625)
                nc.scalar.activation(g3[t][:], a_sb[t][:].indirect(n3_t[:]), COPY, scale=-0.5)
            if t in g4_late:
                g4.append(sb(f"g4_{t}", [P, W], F32, g4_late[t])[:])
                nc.scalar.activation(g4[t], b_sb[t][:].indirect(n4_t[:]), COPY)
            nc.vector.tensor_tensor(a_sb[t][:].indirect(n3_t[:]), g3[t][:], g4[t], ALU.add)
            nc.sync.dma_start(out_rows[:, t, :], a_sb[t][:])
        for t in range(PACK - 1):
            nc.scalar.copy(o_pl[:, t, :], a_sb[t][:])

        o_il = sb("o_il", [P, S, PACK], BF16)
        for copy, c0, c1 in ((nc.vector.tensor_copy, 0, SPLIT), (nc.scalar.copy, SPLIT, S)):
            copy(o_pl[:, 3, c0:c1], a_sb[3][:, c0:c1])
            interleave(copy, o_il, o_pl, c0, c1)
        o_c, o_s = quantize("o", o_il)
        nc.sync.dma_start(out_1[0].rearrange("p n t -> p (n t)").bitcast(I32), o_c[:])
        for q in range(4):
            (nc.scalar if q < 2 else nc.sync).dma_start(out_2[0, 4 * q : 4 * q + 4, :].bitcast(I32), o_s[32 * q : 32 * q + 4, :].bitcast(I32))
